import numpy as np
import ml_dtypes


def mxq(x, axis, fmt="e4m3"):
    dtype, down = {"e4m3": (ml_dtypes.float8_e4m3fn, 7), "e5m2": (ml_dtypes.float8_e5m2, 14)}[fmt]
    v = np.moveaxis(np.asarray(x, np.float32).astype(ml_dtypes.bfloat16).astype(np.float64), axis, -1)
    blocks = v.reshape(v.shape[:-1] + (-1, 32))
    amax = np.abs(blocks).max(-1, keepdims=True)
    byte = np.maximum(np.where(amax > 0, np.frexp(amax)[1] - 1 + 127, 0) - down, 1)
    scale = np.exp2(byte - 127.0)
    codes = (blocks / scale).astype(np.float32).astype(dtype).astype(np.float64)
    return np.moveaxis((codes * scale).reshape(v.shape), -1, axis)


WIDE = False


def mx_kscale(k):
    if not WIDE:
        return np.ones(k)
    levels = np.array([10, -10, 5, -5, 0])
    if k % 512:
        return np.exp2(np.random.permutation(np.resize(levels, k // 32))).repeat(32)
    a = np.empty((k // 512, 16))
    for p in range(k // 512):
        a[p, :8] = np.random.permutation(np.resize(levels, 8))
        for g in range(8):
            far = levels[np.abs(levels - a[p, g]) >= 10]
            a[p, g + 8] = far[np.random.randint(len(far))]
    return np.exp2(a.ravel()).repeat(32)


def f64(x):
    return np.asarray(x).astype(np.float64)


def striped(idx):
    return np.tile(idx.reshape(-1, 16).T, (8, 1)).astype(np.uint16)


def unstriped(offs):
    return offs[:16].T.reshape(-1).astype(np.int64)


def striped8(idx):
    return np.concatenate([x.reshape(-1, 16).T for x in idx]).astype(np.uint16)


def runs(offs, k):
    lists = np.stack([offs[16 * r : 16 * r + 16].T.reshape(-1) for r in range(8)]).astype(np.int64)
    return lists[np.arange(k) % 512 // 64]


def pack_weight(w):
    k, n = w.shape
    w = f64(np.asarray(w, np.float32).astype(ml_dtypes.bfloat16)).reshape(k // 32, 32, n)
    amax = np.abs(w).max(1)
    byte = np.clip(np.where(amax > 0, np.frexp(amax)[1] - 1 + 127 - 7, 1), 1, 254)
    scaled = (w * np.exp2(127.0 - byte)[:, None, :]).reshape(k, n).astype(np.float32)
    words = np.ascontiguousarray(scaled.reshape(k // 512, 128, 4, n).transpose(0, 1, 3, 2)).astype(ml_dtypes.float8_e4m3fn).view(np.uint8)
    return words, np.ascontiguousarray(byte.astype(np.uint8).reshape(k // 512, 16, n))


def unpack_weight(words, scales):
    g, p, n, _ = words.shape
    vals = np.ascontiguousarray(words).view(ml_dtypes.float8_e4m3fn).astype(np.float64) * np.repeat(np.exp2(scales.astype(np.float64) - 127.0), 8, axis=1)[..., None]
    return vals.transpose(0, 1, 3, 2).reshape(g * 512, n)


def sigmoid(v):
    return 1.0 / (1.0 + np.exp(-np.maximum(v, -700.0)))


K, T, S, N, G, H, W = 512, 1024, 512, 512, 2048, 512, 256


def setup_inputs():
    n = np.random.standard_normal
    s = mx_kscale(K)[:, None]
    u = mx_kscale(S)
    packed_xT = pack_weight(n((K, T)) * s)
    packed_dT = pack_weight(n((K, G)) / s)
    perm = np.random.permutation(S)
    return {
        "x_words": packed_xT[0],
        "x_scales": packed_xT[1],
        "d_words": packed_dT[0],
        "d_scales": packed_dT[1],
        "sl": np.random.uniform(1.0, 2.0, (H, 1)).astype(np.float32),
        "th": (0.5 * n((H, 1))).astype(np.float32),
        "gn": (np.random.uniform(0.5, 1.5, (H, 1)) * u[:, None]).astype(np.float32),
        "w1": (n((H, N)) / np.sqrt(2 * H) / u[:, None]).astype(np.float32),
        "w2": (n((K, N)) / np.sqrt(2 * K) / s).astype(np.float32),
        "offs": striped(np.random.permutation(T)[:S]),
        "ci": striped(np.random.permutation(G)[:H]),
        "n1": striped8(np.stack([np.random.permutation(S) for _ in range(8)])),
        "n2": striped8(np.stack([np.random.permutation(S) for _ in range(8)])),
        "two": striped(np.random.permutation(T)[:S]),
        "n3": striped(perm[:W]),
        "n4": striped(perm[W:]),
        "n5": striped(np.random.permutation(S)),
    }


def reference(x_words, x_scales, d_words, d_scales, sl, th, gn, w1, w2, offs, ci, n1, n2, two, n3, n4, n5):
    d_ci = unpack_weight(d_words, d_scales)[:, unstriped(ci)]
    xq = unpack_weight(x_words, x_scales)[:, unstriped(offs)]
    s = 0.0625 * (d_ci.T @ xq)
    sg = sigmoid(f64(sl) * (s[np.arange(H)[:, None], runs(n1, H)] - f64(th)))
    z = f64(gn) * ((s[np.arange(H)[:, None], runs(n2, H)]) * sg)
    x_two = unpack_weight(x_words, x_scales)[:, unstriped(two)]
    h = mxq(f64(w1), 0, "e4m3").T @ mxq(z, 0, "e4m3") + mxq(f64(w2), 0, "e4m3").T @ x_two
    pa = h[:, unstriped(n3)]
    pb = h[:, unstriped(n4)]
    ra = np.maximum(pa, pb)
    ds = h.copy()
    ds[:, unstriped(n3)] = ra
    return ds - ds[:, unstriped(n5)]

@@ -1,0 +1,236 @@
+from contextlib import ExitStack
+
+import concourse.mybir as mybir
+
+K, T, S, N, G, H, W = 512, 1024, 512, 512, 2048, 512, 256
+FLOPS = 2 * (K * H * S + H * N * S + K * N * S)
+
+F32 = mybir.dt.float32
+BF16 = mybir.dt.bfloat16
+I32 = mybir.dt.int32
+U32 = mybir.dt.uint32
+U16 = mybir.dt.uint16
+U8 = mybir.dt.uint8
+FP8X4 = mybir.dt.float8_e4m3fn_x4
+ALU = mybir.AluOpType
+ACT = mybir.ActivationFunctionType
+
+P = 128
+PACK = 4
+HALF = S // 2
+LIST_ROWS = 16
+
+
+def tile_picked_dwmemgfillm_none_p_kernel(
+    tc, x_words, x_scales, d_words, d_scales, sl, th, gn, w1, w2, offs, ci, n1, n2, two, n3, n4, n5, out
+):
+    nc = tc.nc
+    with ExitStack() as ctx:
+        keep = ctx.enter_context(tc.tile_pool(name="keep", bufs=1))
+        psum = ctx.enter_context(tc.psum_pool(name="psum", bufs=1))
+        reuse_d = ctx.enter_context(tc.tile_pool(name="reuse_d", bufs=1))
+        reuse_w2 = ctx.enter_context(tc.tile_pool(name="reuse_w2", bufs=1))
+        reuse_w = ctx.enter_context(tc.tile_pool(name="reuse_w", bufs=1))
+
+        def load_list(name, src):
+            tile = keep.tile(list(src.shape), U16, name=name)
+            nc.sync.dma_start(tile[:], src)
+            return tile
+
+        def load_words(tile, src):
+            nc.sync.dma_start(tile[:], src[0].rearrange("p n t -> p (n t)").bitcast(I32))
+            return tile
+
+        def load_scales(name, src, width, clear, queue):
+            tile = keep.tile([P, width], U8, name=name, align_bytes=64)
+            clear(tile[:].bitcast(I32), 0)
+            for q in range(4):
+                queue.dma_start(
+                    tile[32 * q : 32 * q + 4, :].bitcast(I32), src[0, 4 * q : 4 * q + 4, :].bitcast(I32)
+                )
+            return tile
+
+        def load_rowvec(name, src):
+            tile = keep.tile([P, PACK], F32, name=name)
+            nc.gpsimd.dma_start(tile[:], src.rearrange("(p t) o -> p (t o)", t=PACK))
+            return tile
+
+        def load_weight(tile, src):
+            nc.sync.dma_start(tile[:], src.rearrange("(p t) n -> p t n", t=PACK))
+            return tile
+
+        def half_of(lst, c):
+            cols = HALF // LIST_ROWS
+            return lst[:, c * cols : (c + 1) * cols]
+
+        xs_tab = load_scales("xs_tab", x_scales, T, nc.gpsimd.memset, nc.sync)
+        offs_t = load_list("offs_t", offs)
+        two_t = load_list("two_t", two)
+        xw_tab = load_words(keep.tile([P, T], I32, name="xw_tab", align_bytes=64), x_words)
+        dw_tab = load_words(reuse_d.tile([P, G], I32, name="dw_tab", align_bytes=64, offset=0), d_words)
+        ci_t = load_list("ci_t", ci)
+        ds_tab = load_scales("ds_tab", d_scales, G, nc.vector.memset, nc.sync)
+        n1_t = load_list("n1_t", n1)
+        w1_raw = load_weight(keep.tile([P, PACK, N], F32, name="w1_raw"), w1)
+        n2_t = load_list("n2_t", n2)
+        w2_raw = load_weight(reuse_w2.tile([P, PACK, N], F32, name="w2_raw", offset=0), w2)
+        n3_t = load_list("n3_t", n3)
+        n4_t = load_list("n4_t", n4)
+        n5_t = load_list("n5_t", n5)
+        sl_t = load_rowvec("sl_t", sl)
+        th_t = load_rowvec("th_t", th)
+        gn_t = load_rowvec("gn_t", gn)
+
+        w1_16 = keep.tile([P, N, PACK], BF16, name="w1_16", align_bytes=64)
+        w2_16 = keep.tile([P, N, PACK], BF16, name="w2_16", align_bytes=64)
+        neg_sl = keep.tile([P, PACK], F32, name="neg_sl")
+        bias = keep.tile([P, PACK], F32, name="bias")
+        nc.scalar.activation(neg_sl[:], sl_t[:], ACT.Copy, scale=-1.0)
+        for t in range(PACK):
+            nc.scalar.activation(bias[:, t : t + 1], th_t[:, t : t + 1], ACT.Copy, scale=neg_sl[:, t : t + 1])
+
+        def mx_tiles(name, width):
+            words = keep.tile([P, width], U32, name=name + "_w", align_bytes=64)
+            scales = keep.tile([P, width], U8, name=name + "_s", align_bytes=64)
+            return words, scales
+
+        def pick_words(dst, tab, lst):
+            nc.vector.tensor_copy(dst, tab[:].bitcast(U32).indirect(lst[:]))
+
+        def pick_scales(dst, tab, lst):
+            nc.vector.tensor_copy(dst, tab[:].indirect(lst[:]))
+
+        def dealt(tile):
+            return tile[:].rearrange("p (t m) -> p m t", t=PACK)
+
+        xq_w, xq_s = mx_tiles("xq", S)
+        dq_w, dq_s = mx_tiles("dq", H)
+        x2_s = keep.tile([P, S], U8, name="x2_s", align_bytes=64)
+        pick_scales(xq_s[:], xs_tab, offs_t)
+        pick_words(xq_w[:], xw_tab, offs_t)
+        pick_scales(x2_s[:], xs_tab, two_t)
+        pick_words(dealt(dq_w), dw_tab, ci_t)
+        pick_scales(dealt(dq_s), ds_tab, ci_t)
+
+        s_ps = [psum.tile([P, S], F32, name="s_ps%d" % t) for t in range(PACK)]
+        for t in range(PACK):
+            cols = slice(t * P, (t + 1) * P)
+            nc.tensor.matmul_mx(
+                s_ps[t][:], dq_w[:, cols].bitcast(FP8X4), dq_s[:, cols], xq_w[:].bitcast(FP8X4), xq_s[:],
+                start=True, stop=True,
+            )
+
+        x2_w = reuse_d.tile([P, S], U32, name="x2_w", align_bytes=64, offset=0)
+        pick_words(x2_w[:], xw_tab, two_t)
+
+        def interleave(engine_copy, dst, src):
+            engine_copy(
+                dst.rearrange("p (c i) t -> p c t i", i=4), src.rearrange("p t (c i) -> p c t i", i=4)
+            )
+
+        def quantize(words, scales, grouped):
+            nc.vector.quantize_mx(words[:].bitcast(FP8X4), scales[:], grouped[:].rearrange("p n t -> p (n t)"))
+            return words, scales
+
+        s_sb = [keep.tile([P, S], F32, name="s_sb%d" % t) for t in range(PACK)]
+        gs_sb = [keep.tile([P, S], F32, name="gs_sb%d" % t) for t in range(PACK)]
+        sg = [
+            [keep.tile([P, HALF], F32, name="sg0_%d" % t) for t in range(PACK)],
+            [reuse_w2.tile([P, HALF], F32, name="sg1_%d" % t, offset=4 * HALF * t) for t in range(PACK)],
+        ]
+        z32 = [keep.tile([P, PACK, HALF], F32, name="z32_%d" % c) for c in range(2)]
+        z16 = [keep.tile([P, HALF, PACK], BF16, name="z16_%d" % c, align_bytes=64) for c in range(2)]
+
+        def sigmoid_gather(c, t):
+            nc.scalar.activation(
+                sg[c][t][:], s_sb[t][:].indirect(half_of(n1_t, c)), ACT.Sigmoid,
+                bias=bias[:, t : t + 1], scale=sl_t[:, t : t + 1],
+            )
+
+        def gate_gather(c, t):
+            nc.vector.tensor_tensor(z32[c][:, t, :], gs_sb[t][:].indirect(half_of(n2_t, c)), sg[c][t][:], ALU.mult)
+
+        interleave(nc.vector.tensor_copy, w1_16[:], w1_raw[:])
+        for t in range(PACK):
+            nc.scalar.activation(s_sb[t][:], s_ps[t][:], ACT.Copy, scale=0.0625)
+            sigmoid_gather(0, t)
+            nc.vector.tensor_scalar(gs_sb[t][:], s_sb[t][:], gn_t[:, t : t + 1], None, ALU.mult)
+            gate_gather(0, t)
+
+        interleave(nc.scalar.copy, w2_16[:], w2_raw[:])
+        interleave(nc.vector.tensor_copy, z16[0][:], z32[0][:])
+        w1q_w, w1q_s = quantize(*mx_tiles("w1q", N), w1_16)
+        zq0 = quantize(*mx_tiles("zq0", HALF), z16[0])
+        w2q_w, w2q_s = quantize(*mx_tiles("w2q", N), w2_16)
+
+        h_ps = [psum.tile([P, S], F32, name="h_ps%d" % m) for m in range(4)]
+        for m in range(4):
+            cols = slice(m * P, (m + 1) * P)
+            nc.tensor.matmul_mx(
+                h_ps[m][:], w2q_w[:, cols].bitcast(FP8X4), w2q_s[:, cols], x2_w[:].bitcast(FP8X4), x2_s[:],
+                start=True, stop=False,
+            )
+
+        def w1_pass(c, zq):
+            for m in range(4):
+                cols = slice(m * P, (m + 1) * P)
+                nc.tensor.matmul_mx(
+                    h_ps[m][:, c * HALF : (c + 1) * HALF], w1q_w[:, cols].bitcast(FP8X4), w1q_s[:, cols],
+                    zq[0][:].bitcast(FP8X4), zq[1][:], start=False, stop=(c == 1),
+                )
+
+        w1_pass(0, zq0)
+        for t in range(PACK):
+            sigmoid_gather(1, t)
+            gate_gather(1, t)
+        interleave(nc.vector.tensor_copy, z16[1][:], z32[1][:])
+        w1_pass(1, quantize(*mx_tiles("zq1", HALF), z16[1]))
+
+        ds = [keep.tile([P, S], F32, name="ds%d" % m) for m in range(2)]
+        ds = ds + [reuse_w.tile([P, S], F32, name="ds%d" % (m + 2), offset=4 * S * m) for m in range(2)]
+        neg = [keep.tile([P, S], F32, name="neg%d" % m) for m in range(4)]
+        res = [keep.tile([P, S], F32, name="res%d" % m) for m in range(4)]
+        pa = [reuse_w.tile([P, W], F32, name="pa%d" % m, offset=4 * S * m) for m in range(2)]
+        pb = [reuse_w.tile([P, W], F32, name="pb%d" % m, offset=4 * S * m + 4 * W) for m in range(2)]
+        pa = pa + [keep.tile([P, W], F32, name="pa%d" % m) for m in (2, 3)]
+        pb = pb + [keep.tile([P, W], F32, name="pb%d" % m) for m in (2, 3)]
+        ra = [keep.tile([P, W], F32, name="ra%d" % m) for m in range(4)]
+
+        def pair_up(m):
+            if m == 0:
+                nc.scalar.copy(ds[m][:], h_ps[m][:])
+            else:
+                nc.vector.tensor_copy(ds[m][:], h_ps[m][:])
+            if m < 2:
+                nc.scalar.activation(pa[m][:], ds[m][:].indirect(n3_t[:]), ACT.Copy)
+            else:
+                nc.vector.tensor_copy(pa[m][:], ds[m][:].indirect(n3_t[:]))
+            nc.vector.tensor_copy(pb[m][:], ds[m][:].indirect(n4_t[:]))
+            nc.vector.tensor_tensor(ra[m][:], pa[m][:], pb[m][:], ALU.max)
+
+        def put_back(m):
+            nc.scalar.activation(ds[m][:].indirect(n3_t[:]), ra[m][:], ACT.Copy)
+
+        def finish(m):
+            if m < 2:
+                nc.vector.tensor_scalar(neg[m][:], ds[m][:], -1.0, None, ALU.mult)
+            for c in range(2):
+                cols = slice(c * HALF, (c + 1) * HALF)
+                if m < 2:
+                    nc.vector.tensor_tensor(
+                        res[m][:, cols], neg[m][:].indirect(half_of(n5_t, c)), ds[m][:, cols], ALU.add
+                    )
+                else:
+                    nc.scalar.activation(neg[m][:, cols], ds[m][:].indirect(half_of(n5_t, c)), ACT.Copy)
+                    nc.vector.tensor_tensor(res[m][:, cols], ds[m][:, cols], neg[m][:, cols], ALU.subtract)
+                if m == 3:
+                    nc.sync.dma_start(out[m * P : (m + 1) * P, cols], res[m][:, cols])
+            if m < 3:
+                nc.sync.dma_start(out[m * P : (m + 1) * P, :], res[m][:])
+
+        for m in range(4):
+            pair_up(m)
+        for m in range(4):
+            put_back(m)
+        for m in range(4):
+            finish(m)

@@ -41,8 +41,7 @@ def tile_picked_dwmemgfillm_none_p_kernel(
             nc.sync.dma_start(tile[:], src[0].rearrange("p n t -> p (n t)").bitcast(I32))
             return tile
 
-        def load_scales(name, src, width, clear, queue):
-            tile = keep.tile([P, width], U8, name=name, align_bytes=64)
+        def load_scales(tile, src, clear, queue):
             clear(tile[:].bitcast(I32), 0)
             for q in range(4):
                 queue.dma_start(
@@ -63,13 +62,13 @@ def tile_picked_dwmemgfillm_none_p_kernel(
             cols = HALF // LIST_ROWS
             return lst[:, c * cols : (c + 1) * cols]
 
-        xs_tab = load_scales("xs_tab", x_scales, T, nc.gpsimd.memset, nc.sync)
+        xs_tab = load_scales(keep.tile([P, T], U8, name="xs_tab", align_bytes=64), x_scales, nc.gpsimd.memset, nc.sync)
         offs_t = load_list("offs_t", offs)
         two_t = load_list("two_t", two)
         xw_tab = load_words(keep.tile([P, T], I32, name="xw_tab", align_bytes=64), x_words)
         dw_tab = load_words(reuse_d.tile([P, G], I32, name="dw_tab", align_bytes=64, offset=0), d_words)
         ci_t = load_list("ci_t", ci)
-        ds_tab = load_scales("ds_tab", d_scales, G, nc.vector.memset, nc.sync)
+        ds_tab = load_scales(reuse_d.tile([P, G], U8, name="ds_tab", align_bytes=64, offset=4 * G), d_scales, nc.vector.memset, nc.sync)
         n1_t = load_list("n1_t", n1)
         w1_raw = load_weight(keep.tile([P, PACK, N], F32, name="w1_raw"), w1)
         n2_t = load_list("n2_t", n2)
@@ -85,6 +84,9 @@ def tile_picked_dwmemgfillm_none_p_kernel(
         w2_16 = keep.tile([P, N, PACK], BF16, name="w2_16", align_bytes=64)
         neg_sl = keep.tile([P, PACK], F32, name="neg_sl")
         bias = keep.tile([P, PACK], F32, name="bias")
+        warm = keep.tile([P, 2], F32, name="warm")
+        nc.vector.memset(warm[:, 0:1], 0.0)
+        nc.scalar.activation(warm[:, 1:2], warm[:, 0:1], ACT.Sigmoid)
         nc.scalar.activation(neg_sl[:], sl_t[:], ACT.Copy, scale=-1.0)
         for t in range(PACK):
             nc.scalar.activation(bias[:, t : t + 1], th_t[:, t : t + 1], ACT.Copy, scale=neg_sl[:, t : t + 1])
@@ -120,7 +122,7 @@ def tile_picked_dwmemgfillm_none_p_kernel(
                 start=True, stop=True,
             )
 
-        x2_w = reuse_d.tile([P, S], U32, name="x2_w", align_bytes=64, offset=0)
+        x2_w = reuse_d.tile([P, S], U32, name="x2_w", align_bytes=64, offset=4 * G - 2 * S)
         pick_words(x2_w[:], xw_tab, two_t)
 
         def interleave(engine_copy, dst, src):
@@ -188,49 +190,85 @@ def tile_picked_dwmemgfillm_none_p_kernel(
 
         ds = [keep.tile([P, S], F32, name="ds%d" % m) for m in range(2)]
         ds = ds + [reuse_w.tile([P, S], F32, name="ds%d" % (m + 2), offset=4 * S * m) for m in range(2)]
-        neg = [keep.tile([P, S], F32, name="neg%d" % m) for m in range(4)]
         res = [keep.tile([P, S], F32, name="res%d" % m) for m in range(4)]
         pa = [reuse_w.tile([P, W], F32, name="pa%d" % m, offset=4 * S * m) for m in range(2)]
-        pb = [reuse_w.tile([P, W], F32, name="pb%d" % m, offset=4 * S * m + 4 * W) for m in range(2)]
+        pb = [reuse_w.tile([P, W], F32, name="pb%d" % m, offset=8 * S) for m in range(2)]
         pa = pa + [keep.tile([P, W], F32, name="pa%d" % m) for m in (2, 3)]
         pb = pb + [keep.tile([P, W], F32, name="pb%d" % m) for m in (2, 3)]
-        ra = [keep.tile([P, W], F32, name="ra%d" % m) for m in range(4)]
+        ra = [keep.tile([P, W], F32, name="ra%d" % m) for m in range(3)]
+        ra = ra + [reuse_w.tile([P, W], F32, name="ra3", offset=10 * S)]
+        neg = [keep.tile([P, S], F32, name="neg%d" % m) for m in range(2)]
+        moved = [reuse_w.tile([P, S], F32, name="moved2", offset=10 * S), keep.tile([P, S], F32, name="moved3")]
+        halves = [slice(c * HALF, (c + 1) * HALF) for c in range(2)]
 
-        def pair_up(m):
-            if m == 0:
-                nc.scalar.copy(ds[m][:], h_ps[m][:])
-            else:
-                nc.vector.tensor_copy(ds[m][:], h_ps[m][:])
-            if m < 2:
-                nc.scalar.activation(pa[m][:], ds[m][:].indirect(n3_t[:]), ACT.Copy)
-            else:
-                nc.vector.tensor_copy(pa[m][:], ds[m][:].indirect(n3_t[:]))
-            nc.vector.tensor_copy(pb[m][:], ds[m][:].indirect(n4_t[:]))
+        def on_scalar(dst, src):
+            nc.scalar.activation(dst, src, ACT.Copy)
+
+        on_vector = nc.vector.tensor_copy
+
+        def leave_psum(m, copy):
+            copy(ds[m][:], h_ps[m][:])
+
+        def fetch_pa(m, copy):
+            copy(pa[m][:], ds[m][:].indirect(n3_t[:]))
+
+        def fetch_pb(m):
+            on_vector(pb[m][:], ds[m][:].indirect(n4_t[:]))
+
+        def larger(m):
             nc.vector.tensor_tensor(ra[m][:], pa[m][:], pb[m][:], ALU.max)
 
         def put_back(m):
-            nc.scalar.activation(ds[m][:].indirect(n3_t[:]), ra[m][:], ACT.Copy)
+            on_scalar(ds[m][:].indirect(n3_t[:]), ra[m][:])
 
-        def finish(m):
-            if m < 2:
-                nc.vector.tensor_scalar(neg[m][:], ds[m][:], -1.0, None, ALU.mult)
+        def negate(m):
+            nc.vector.tensor_scalar(neg[m][:], ds[m][:], -1.0, None, ALU.mult)
+
+        def fused_difference(m):
             for c in range(2):
-                cols = slice(c * HALF, (c + 1) * HALF)
-                if m < 2:
-                    nc.vector.tensor_tensor(
-                        res[m][:, cols], neg[m][:].indirect(half_of(n5_t, c)), ds[m][:, cols], ALU.add
-                    )
-                else:
-                    nc.scalar.activation(neg[m][:, cols], ds[m][:].indirect(half_of(n5_t, c)), ACT.Copy)
-                    nc.vector.tensor_tensor(res[m][:, cols], ds[m][:, cols], neg[m][:, cols], ALU.subtract)
-                if m == 3:
-                    nc.sync.dma_start(out[m * P : (m + 1) * P, cols], res[m][:, cols])
-            if m < 3:
-                nc.sync.dma_start(out[m * P : (m + 1) * P, :], res[m][:])
+                nc.vector.tensor_tensor(
+                    res[m][:, halves[c]], neg[m][:].indirect(half_of(n5_t, c)), ds[m][:, halves[c]], ALU.add
+                )
 
-        for m in range(4):
-            pair_up(m)
-        for m in range(4):
-            put_back(m)
-        for m in range(4):
-            finish(m)
+        def fetch_moved(m, c, copy):
+            copy(moved[m - 2][:, halves[c]], ds[m][:].indirect(half_of(n5_t, c)))
+
+        def difference(m, cols):
+            nc.vector.tensor_tensor(res[m][:, cols], ds[m][:, cols], moved[m - 2][:, cols], ALU.subtract)
+
+        def store(m, cols):
+            nc.sync.dma_start(out[m * P : (m + 1) * P, cols], res[m][:, cols])
+
+        whole = slice(0, S)
+        leave_psum(0, nc.scalar.copy)
+        leave_psum(1, on_vector)
+        fetch_pa(0, on_scalar)
+        fetch_pb(0)
+        larger(0)
+        fetch_pa(1, on_scalar)
+        fetch_pb(1)
+        put_back(0)
+        leave_psum(2, on_vector)
+        larger(1)
+        fetch_pa(2, on_scalar)
+        fetch_pb(2)
+        put_back(1)
+        leave_psum(3, on_vector)
+        larger(2)
+        put_back(2)
+        fetch_pa(3, on_vector)
+        fetch_pb(3)
+        larger(3)
+        put_back(3)
+        for m in range(2):
+            negate(m)
+            fused_difference(m)
+            store(m, whole)
+        fetch_moved(2, 0, on_scalar)
+        fetch_moved(2, 1, on_vector)
+        difference(2, whole)
+        store(2, whole)
+        for c in range(2):
+            fetch_moved(3, c, on_scalar)
+            difference(3, halves[c])
+            store(3, halves[c])

@@ -17,8 +17,13 @@ ACT = mybir.ActivationFunctionType
 
 P = 128
 PACK = 4
-HALF = S // 2
+QUADRANT = 32
+ROW_TILES = N // P
 LIST_ROWS = 16
+HALF = S // 2
+ROW_BYTES = 4 * S
+LINE = 4
+W1_TILES_ON_VECTOR = 2
 
 
 def tile_picked_dwmemgfillm_none_p_kernel(
@@ -28,9 +33,9 @@ def tile_picked_dwmemgfillm_none_p_kernel(
     with ExitStack() as ctx:
         keep = ctx.enter_context(tc.tile_pool(name="keep", bufs=1))
         psum = ctx.enter_context(tc.psum_pool(name="psum", bufs=1))
-        reuse_d = ctx.enter_context(tc.tile_pool(name="reuse_d", bufs=1))
-        reuse_w2 = ctx.enter_context(tc.tile_pool(name="reuse_w2", bufs=1))
-        reuse_w = ctx.enter_context(tc.tile_pool(name="reuse_w", bufs=1))
+        dict_pool = ctx.enter_context(tc.tile_pool(name="dict_pool", bufs=1))
+        score_pool = ctx.enter_context(tc.tile_pool(name="score_pool", bufs=1))
+        pair_pool = ctx.enter_context(tc.tile_pool(name="pair_pool", bufs=1))
 
         def load_list(name, src):
             tile = keep.tile(list(src.shape), U16, name=name)
@@ -41,52 +46,51 @@ def tile_picked_dwmemgfillm_none_p_kernel(
             nc.sync.dma_start(tile[:], src[0].rearrange("p n t -> p (n t)").bitcast(I32))
             return tile
 
-        def load_scales(tile, src, clear, queue):
-            clear(tile[:].bitcast(I32), 0)
-            for q in range(4):
-                queue.dma_start(
-                    tile[32 * q : 32 * q + 4, :].bitcast(I32), src[0, 4 * q : 4 * q + 4, :].bitcast(I32)
-                )
+        def load_scales(tile, src, memset):
+            memset(tile[:].bitcast(I32), 0)
+            for q in range(P // QUADRANT):
+                rows = src[0, PACK * q : PACK * (q + 1), :]
+                nc.sync.dma_start(tile[QUADRANT * q : QUADRANT * q + PACK, :].bitcast(I32), rows.bitcast(I32))
             return tile
 
-        def load_rowvec(name, src):
+        def load_by_slot(name, src):
             tile = keep.tile([P, PACK], F32, name=name)
             nc.gpsimd.dma_start(tile[:], src.rearrange("(p t) o -> p (t o)", t=PACK))
             return tile
 
-        def load_weight(tile, src):
-            nc.sync.dma_start(tile[:], src.rearrange("(p t) n -> p t n", t=PACK))
-            return tile
+        def load_weight(dst, src):
+            nc.sync.dma_start(dst, src.rearrange("(p t) n -> p t n", t=PACK))
 
         def half_of(lst, c):
             cols = HALF // LIST_ROWS
             return lst[:, c * cols : (c + 1) * cols]
 
-        xs_tab = load_scales(keep.tile([P, T], U8, name="xs_tab", align_bytes=64), x_scales, nc.gpsimd.memset, nc.sync)
+        xs_tab = load_scales(keep.tile([P, T], U8, name="xs_tab", align_bytes=64), x_scales, nc.gpsimd.memset)
         offs_t = load_list("offs_t", offs)
         two_t = load_list("two_t", two)
         xw_tab = load_words(keep.tile([P, T], I32, name="xw_tab", align_bytes=64), x_words)
-        dw_tab = load_words(reuse_d.tile([P, G], I32, name="dw_tab", align_bytes=64, offset=0), d_words)
+        dw_tab = load_words(dict_pool.tile([P, G], I32, name="dw_tab", align_bytes=64, offset=0), d_words)
         ci_t = load_list("ci_t", ci)
-        ds_tab = load_scales(reuse_d.tile([P, G], U8, name="ds_tab", align_bytes=64, offset=4 * G), d_scales, nc.vector.memset, nc.sync)
+        ds_tab = dict_pool.tile([P, G], U8, name="ds_tab", align_bytes=64, offset=4 * G)
+        load_scales(ds_tab, d_scales, nc.vector.memset)
         n1_t = load_list("n1_t", n1)
-        w1_raw = load_weight(keep.tile([P, PACK, N], F32, name="w1_raw"), w1)
+        w_raw = keep.tile([P, 2, PACK, N], F32, name="w_raw")
+        load_weight(w_raw[:, 0], w1)
         n2_t = load_list("n2_t", n2)
-        w2_raw = load_weight(reuse_w2.tile([P, PACK, N], F32, name="w2_raw", offset=0), w2)
+        load_weight(w_raw[:, 1], w2)
         n3_t = load_list("n3_t", n3)
         n4_t = load_list("n4_t", n4)
         n5_t = load_list("n5_t", n5)
-        sl_t = load_rowvec("sl_t", sl)
-        th_t = load_rowvec("th_t", th)
-        gn_t = load_rowvec("gn_t", gn)
+        sl_t = load_by_slot("sl_t", sl)
+        th_t = load_by_slot("th_t", th)
+        gn_t = load_by_slot("gn_t", gn)
 
-        w1_16 = keep.tile([P, N, PACK], BF16, name="w1_16", align_bytes=64)
-        w2_16 = keep.tile([P, N, PACK], BF16, name="w2_16", align_bytes=64)
-        neg_sl = keep.tile([P, PACK], F32, name="neg_sl")
-        bias = keep.tile([P, PACK], F32, name="bias")
         warm = keep.tile([P, 2], F32, name="warm")
         nc.vector.memset(warm[:, 0:1], 0.0)
         nc.scalar.activation(warm[:, 1:2], warm[:, 0:1], ACT.Sigmoid)
+
+        neg_sl = keep.tile([P, PACK], F32, name="neg_sl")
+        bias = keep.tile([P, PACK], F32, name="bias")
         nc.scalar.activation(neg_sl[:], sl_t[:], ACT.Copy, scale=-1.0)
         for t in range(PACK):
             nc.scalar.activation(bias[:, t : t + 1], th_t[:, t : t + 1], ACT.Copy, scale=neg_sl[:, t : t + 1])
@@ -103,7 +107,7 @@ def tile_picked_dwmemgfillm_none_p_kernel(
             nc.vector.tensor_copy(dst, tab[:].indirect(lst[:]))
 
         def dealt(tile):
-            return tile[:].rearrange("p (t m) -> p m t", t=PACK)
+            return tile[:].rearrange("q (t p) -> q p t", t=PACK)
 
         xq_w, xq_s = mx_tiles("xq", S)
         dq_w, dq_s = mx_tiles("dq", H)
@@ -122,153 +126,140 @@ def tile_picked_dwmemgfillm_none_p_kernel(
                 start=True, stop=True,
             )
 
-        x2_w = reuse_d.tile([P, S], U32, name="x2_w", align_bytes=64, offset=4 * G - 2 * S)
+        x2_w = dict_pool.tile([P, S], U32, name="x2_w", align_bytes=64, offset=4 * G - ROW_BYTES // 2)
         pick_words(x2_w[:], xw_tab, two_t)
 
-        def interleave(engine_copy, dst, src):
-            engine_copy(
-                dst.rearrange("p (c i) t -> p c t i", i=4), src.rearrange("p t (c i) -> p c t i", i=4)
-            )
-
-        def quantize(words, scales, grouped):
-            nc.vector.quantize_mx(words[:].bitcast(FP8X4), scales[:], grouped[:].rearrange("p n t -> p (n t)"))
+        def quantize(name, woven, width):
+            words, scales = mx_tiles(name, width)
+            nc.vector.quantize_mx(words[:].bitcast(FP8X4), scales[:], woven)
             return words, scales
-
-        s_sb = [keep.tile([P, S], F32, name="s_sb%d" % t) for t in range(PACK)]
-        gs_sb = [keep.tile([P, S], F32, name="gs_sb%d" % t) for t in range(PACK)]
-        sg = [
-            [keep.tile([P, HALF], F32, name="sg0_%d" % t) for t in range(PACK)],
-            [reuse_w2.tile([P, HALF], F32, name="sg1_%d" % t, offset=4 * HALF * t) for t in range(PACK)],
-        ]
-        z32 = [keep.tile([P, PACK, HALF], F32, name="z32_%d" % c) for c in range(2)]
-        z16 = [keep.tile([P, HALF, PACK], BF16, name="z16_%d" % c, align_bytes=64) for c in range(2)]
-
-        def sigmoid_gather(c, t):
-            nc.scalar.activation(
-                sg[c][t][:], s_sb[t][:].indirect(half_of(n1_t, c)), ACT.Sigmoid,
-                bias=bias[:, t : t + 1], scale=sl_t[:, t : t + 1],
-            )
-
-        def gate_gather(c, t):
-            nc.vector.tensor_tensor(z32[c][:, t, :], gs_sb[t][:].indirect(half_of(n2_t, c)), sg[c][t][:], ALU.mult)
-
-        interleave(nc.vector.tensor_copy, w1_16[:], w1_raw[:])
-        for t in range(PACK):
-            nc.scalar.activation(s_sb[t][:], s_ps[t][:], ACT.Copy, scale=0.0625)
-            sigmoid_gather(0, t)
-            nc.vector.tensor_scalar(gs_sb[t][:], s_sb[t][:], gn_t[:, t : t + 1], None, ALU.mult)
-            gate_gather(0, t)
-
-        interleave(nc.scalar.copy, w2_16[:], w2_raw[:])
-        interleave(nc.vector.tensor_copy, z16[0][:], z32[0][:])
-        w1q_w, w1q_s = quantize(*mx_tiles("w1q", N), w1_16)
-        zq0 = quantize(*mx_tiles("zq0", HALF), z16[0])
-        w2q_w, w2q_s = quantize(*mx_tiles("w2q", N), w2_16)
-
-        h_ps = [psum.tile([P, S], F32, name="h_ps%d" % m) for m in range(4)]
-        for m in range(4):
-            cols = slice(m * P, (m + 1) * P)
-            nc.tensor.matmul_mx(
-                h_ps[m][:], w2q_w[:, cols].bitcast(FP8X4), w2q_s[:, cols], x2_w[:].bitcast(FP8X4), x2_s[:],
-                start=True, stop=False,
-            )
-
-        def w1_pass(c, zq):
-            for m in range(4):
-                cols = slice(m * P, (m + 1) * P)
-                nc.tensor.matmul_mx(
-                    h_ps[m][:, c * HALF : (c + 1) * HALF], w1q_w[:, cols].bitcast(FP8X4), w1q_s[:, cols],
-                    zq[0][:].bitcast(FP8X4), zq[1][:], start=False, stop=(c == 1),
-                )
-
-        w1_pass(0, zq0)
-        for t in range(PACK):
-            sigmoid_gather(1, t)
-            gate_gather(1, t)
-        interleave(nc.vector.tensor_copy, z16[1][:], z32[1][:])
-        w1_pass(1, quantize(*mx_tiles("zq1", HALF), z16[1]))
-
-        ds = [keep.tile([P, S], F32, name="ds%d" % m) for m in range(2)]
-        ds = ds + [reuse_w.tile([P, S], F32, name="ds%d" % (m + 2), offset=4 * S * m) for m in range(2)]
-        res = [keep.tile([P, S], F32, name="res%d" % m) for m in range(4)]
-        pa = [reuse_w.tile([P, W], F32, name="pa%d" % m, offset=4 * S * m) for m in range(2)]
-        pb = [reuse_w.tile([P, W], F32, name="pb%d" % m, offset=8 * S) for m in range(2)]
-        pa = pa + [keep.tile([P, W], F32, name="pa%d" % m) for m in (2, 3)]
-        pb = pb + [keep.tile([P, W], F32, name="pb%d" % m) for m in (2, 3)]
-        ra = [keep.tile([P, W], F32, name="ra%d" % m) for m in range(3)]
-        ra = ra + [reuse_w.tile([P, W], F32, name="ra3", offset=10 * S)]
-        neg = [keep.tile([P, S], F32, name="neg%d" % m) for m in range(2)]
-        moved = [reuse_w.tile([P, S], F32, name="moved2", offset=10 * S), keep.tile([P, S], F32, name="moved3")]
-        halves = [slice(c * HALF, (c + 1) * HALF) for c in range(2)]
 
         def on_scalar(dst, src):
             nc.scalar.activation(dst, src, ACT.Copy)
 
         on_vector = nc.vector.tensor_copy
 
-        def leave_psum(m, copy):
-            copy(ds[m][:], h_ps[m][:])
+        def score_tile(name, shape, dtype, place):
+            return score_pool.tile(shape, dtype, name=name, align_bytes=64, offset=place * ROW_BYTES)
 
-        def fetch_pa(m, copy):
-            copy(pa[m][:], ds[m][:].indirect(n3_t[:]))
+        s_sb = [score_tile("s_sb%d" % t, [P, S], F32, t) for t in range(PACK)]
+        gs_sb = [keep.tile([P, S], F32, name="gs_sb%d" % t) for t in range(PACK)]
+        sg = [[keep.tile([P, HALF], F32, name="sg%d_%d" % (c, t)) for t in range(PACK)] for c in range(2)]
+        z32 = [keep.tile([P, PACK, HALF], F32, name="z32_%d" % c) for c in range(2)]
 
-        def fetch_pb(m):
-            on_vector(pb[m][:], ds[m][:].indirect(n4_t[:]))
+        def gate(c, t):
+            nc.scalar.activation(
+                sg[c][t][:], s_sb[t][:].indirect(half_of(n1_t, c)), ACT.Sigmoid,
+                bias=bias[:, t : t + 1], scale=sl_t[:, t : t + 1],
+            )
 
-        def larger(m):
-            nc.vector.tensor_tensor(ra[m][:], pa[m][:], pb[m][:], ALU.max)
+        def gated_score(c, t):
+            nc.vector.tensor_tensor(z32[c][:, t, :], gs_sb[t][:].indirect(half_of(n2_t, c)), sg[c][t][:], ALU.mult)
+
+        def round_z(c, z16):
+            on_vector(
+                z16[:].rearrange("p (g i) t -> p g t i", i=LINE), z32[c][:].rearrange("p t (g i) -> p g t i", i=LINE)
+            )
+
+        w16_place = [PACK + m if m < W1_TILES_ON_VECTOR else m for m in range(ROW_TILES)]
+        w16 = [score_tile("w16_%d" % m, [P, 2, P, PACK], BF16, w16_place[m]) for m in range(ROW_TILES)]
+        h_ps = [psum.tile([P, S], F32, name="h_ps%d" % m) for m in range(ROW_TILES)]
+        wq = []
+
+        def round_weights(m, which, copy):
+            copy(
+                w16[m][:, which].rearrange("p w (g i) t -> p w g t i", i=LINE),
+                w_raw[:, which, :, m * P : (m + 1) * P].rearrange("p w t (g i) -> p w g t i", i=LINE),
+            )
+
+        only_w1, only_w2, both = slice(0, 1), slice(1, 2), slice(0, 2)
+        for m in range(W1_TILES_ON_VECTOR):
+            round_weights(m, only_w1, on_vector)
+
+        for t in range(PACK):
+            nc.scalar.activation(s_sb[t][:], s_ps[t][:], ACT.Copy, scale=0.0625)
+            gate(0, t)
+            nc.vector.tensor_scalar(gs_sb[t][:], s_sb[t][:], gn_t[:, t : t + 1], None, ALU.mult)
+            gated_score(0, t)
+
+        z16_lo = keep.tile([P, HALF, PACK], BF16, name="z16_lo", align_bytes=64)
+        round_z(0, z16_lo)
+        gate(1, 0)
+        gated_score(1, 0)
+        zq = [quantize("zq0", z16_lo[:].rearrange("p j t -> p (j t)"), HALF)]
+        for t in range(1, PACK):
+            gate(1, t)
+            gated_score(1, t)
+
+        def w1_pass(m, c):
+            words, scales = wq[m]
+            nc.tensor.matmul_mx(
+                h_ps[m][:, c * HALF : (c + 1) * HALF], words[:, :P].bitcast(FP8X4), scales[:, :P],
+                zq[c][0][:].bitcast(FP8X4), zq[c][1][:], start=False, stop=(c == 1),
+            )
+
+        def open_group(m):
+            wq.append(quantize("wq%d" % m, w16[m][:].rearrange("p w c t -> p (w c t)"), 2 * P))
+            words, scales = wq[m]
+            nc.tensor.matmul_mx(
+                h_ps[m][:], words[:, P:].bitcast(FP8X4), scales[:, P:], x2_w[:].bitcast(FP8X4), x2_s[:],
+                start=True, stop=False,
+            )
+            w1_pass(m, 0)
+
+        for m in range(ROW_TILES):
+            round_weights(m, only_w2 if m < W1_TILES_ON_VECTOR else both, nc.scalar.copy)
+        open_group(0)
+        z16_hi = score_tile("z16_hi", [P, HALF, PACK], BF16, w16_place[0])
+        round_z(1, z16_hi)
+        zq.append(quantize("zq1", z16_hi[:].rearrange("p j t -> p (j t)"), HALF))
+        w1_pass(0, 1)
+        last = ROW_TILES - 1
+        for m in range(1, last):
+            open_group(m)
+            w1_pass(m, 1)
+
+        early, late = range(2), range(2, ROW_TILES)
+        ds = [keep.tile([P, S], F32, name="ds%d" % m) for m in early]
+        ds = ds + [pair_pool.tile([P, S], F32, name="ds%d" % m, offset=(m - 2) * ROW_BYTES) for m in late]
+        res = [keep.tile([P, S], F32, name="res%d" % m) for m in range(ROW_TILES)]
+        pa = [pair_pool.tile([P, W], F32, name="pa%d" % m, offset=m * ROW_BYTES) for m in early]
+        pb = [pair_pool.tile([P, W], F32, name="pb%d" % m, offset=2 * ROW_BYTES) for m in early]
+        pa = pa + [keep.tile([P, W], F32, name="pa%d" % m) for m in late]
+        pb = pb + [keep.tile([P, W], F32, name="pb%d" % m) for m in late]
+        ra = [keep.tile([P, W], F32, name="ra%d" % m) for m in range(ROW_TILES)]
+        neg_ds = [keep.tile([P, S], F32, name="neg_ds%d" % m) for m in range(last)]
+        ds_n5 = keep.tile([P, S], F32, name="ds_n5")
+        halves = [slice(c * HALF, (c + 1) * HALF) for c in range(2)]
 
         def put_back(m):
             on_scalar(ds[m][:].indirect(n3_t[:]), ra[m][:])
 
-        def negate(m):
-            nc.vector.tensor_scalar(neg[m][:], ds[m][:], -1.0, None, ALU.mult)
-
-        def fused_difference(m):
-            for c in range(2):
-                nc.vector.tensor_tensor(
-                    res[m][:, halves[c]], neg[m][:].indirect(half_of(n5_t, c)), ds[m][:, halves[c]], ALU.add
-                )
-
-        def fetch_moved(m, c, copy):
-            copy(moved[m - 2][:, halves[c]], ds[m][:].indirect(half_of(n5_t, c)))
-
-        def difference(m, cols):
-            nc.vector.tensor_tensor(res[m][:, cols], ds[m][:, cols], moved[m - 2][:, cols], ALU.subtract)
-
         def store(m, cols):
             nc.sync.dma_start(out[m * P : (m + 1) * P, cols], res[m][:, cols])
 
-        whole = slice(0, S)
-        leave_psum(0, nc.scalar.copy)
-        leave_psum(1, on_vector)
-        fetch_pa(0, on_scalar)
-        fetch_pb(0)
-        larger(0)
-        fetch_pa(1, on_scalar)
-        fetch_pb(1)
-        put_back(0)
-        leave_psum(2, on_vector)
-        larger(1)
-        fetch_pa(2, on_scalar)
-        fetch_pb(2)
-        put_back(1)
-        leave_psum(3, on_vector)
-        larger(2)
-        put_back(2)
-        fetch_pa(3, on_vector)
-        fetch_pb(3)
-        larger(3)
-        put_back(3)
-        for m in range(2):
-            negate(m)
-            fused_difference(m)
-            store(m, whole)
-        fetch_moved(2, 0, on_scalar)
-        fetch_moved(2, 1, on_vector)
-        difference(2, whole)
-        store(2, whole)
+        on_vector(ds[0][:], h_ps[0][:])
+        open_group(last)
+        w1_pass(last, 1)
+        for m in range(ROW_TILES):
+            on_scalar(pa[m][:], ds[m][:].indirect(n3_t[:]))
+            if m > 0:
+                put_back(m - 1)
+            if m < last:
+                copy = nc.scalar.copy if m == 0 else on_vector
+                copy(ds[m + 1][:], h_ps[m + 1][:])
+            on_vector(pb[m][:], ds[m][:].indirect(n4_t[:]))
+            nc.vector.tensor_tensor(ra[m][:], pa[m][:], pb[m][:], ALU.max)
+        put_back(last)
+
+        for m in range(last):
+            nc.vector.tensor_scalar(neg_ds[m][:], ds[m][:], -1.0, None, ALU.mult)
+            for c in range(2):
+                nc.vector.tensor_tensor(
+                    res[m][:, halves[c]], neg_ds[m][:].indirect(half_of(n5_t, c)), ds[m][:, halves[c]], ALU.add
+                )
+            store(m, slice(0, S))
         for c in range(2):
-            fetch_moved(3, c, on_scalar)
-            difference(3, halves[c])
-            store(3, halves[c])
+            on_scalar(ds_n5[:, halves[c]], ds[last][:].indirect(half_of(n5_t, c)))
+            nc.vector.tensor_tensor(res[last][:, halves[c]], ds[last][:, halves[c]], ds_n5[:, halves[c]], ALU.subtract)
+            store(last, halves[c])

from contextlib import ExitStack

import concourse.mybir as mybir

K, T, S, N, G, H, W = 512, 1024, 512, 512, 2048, 512, 256
FLOPS = 2 * (K * H * S + H * N * S + K * N * S)

F32 = mybir.dt.float32
BF16 = mybir.dt.bfloat16
I32 = mybir.dt.int32
U32 = mybir.dt.uint32
U16 = mybir.dt.uint16
U8 = mybir.dt.uint8
FP8X4 = mybir.dt.float8_e4m3fn_x4
ALU = mybir.AluOpType
ACT = mybir.ActivationFunctionType

P = 128
PACK = 4
QUADRANT = 32
ROW_TILES = N // P
LIST_ROWS = 16
HALF = S // 2
ROW_BYTES = 4 * S
LINE = 4
W1_TILES_ON_VECTOR = 2


def tile_picked_dwmemgfillm_none_p_kernel(
    tc, x_words, x_scales, d_words, d_scales, sl, th, gn, w1, w2, offs, ci, n1, n2, two, n3, n4, n5, out
):
    nc = tc.nc
    with ExitStack() as ctx:
        keep = ctx.enter_context(tc.tile_pool(name="keep", bufs=1))
        psum = ctx.enter_context(tc.psum_pool(name="psum", bufs=1))
        dict_pool = ctx.enter_context(tc.tile_pool(name="dict_pool", bufs=1))
        score_pool = ctx.enter_context(tc.tile_pool(name="score_pool", bufs=1))
        pair_pool = ctx.enter_context(tc.tile_pool(name="pair_pool", bufs=1))

        def load_list(name, src):
            tile = keep.tile(list(src.shape), U16, name=name)
            nc.sync.dma_start(tile[:], src)
            return tile

        def load_words(tile, src):
            nc.sync.dma_start(tile[:], src[0].rearrange("p n t -> p (n t)").bitcast(I32))
            return tile

        def load_scales(tile, src, memset):
            memset(tile[:].bitcast(I32), 0)
            for q in range(P // QUADRANT):
                rows = src[0, PACK * q : PACK * (q + 1), :]
                nc.sync.dma_start(tile[QUADRANT * q : QUADRANT * q + PACK, :].bitcast(I32), rows.bitcast(I32))
            return tile

        def load_by_slot(name, src):
            tile = keep.tile([P, PACK], F32, name=name)
            nc.gpsimd.dma_start(tile[:], src.rearrange("(p t) o -> p (t o)", t=PACK))
            return tile

        def load_weight(dst, src):
            nc.sync.dma_start(dst, src.rearrange("(p t) n -> p t n", t=PACK))

        def half_of(lst, c):
            cols = HALF // LIST_ROWS
            return lst[:, c * cols : (c + 1) * cols]

        xs_tab = load_scales(keep.tile([P, T], U8, name="xs_tab", align_bytes=64), x_scales, nc.gpsimd.memset)
        offs_t = load_list("offs_t", offs)
        two_t = load_list("two_t", two)
        xw_tab = load_words(keep.tile([P, T], I32, name="xw_tab", align_bytes=64), x_words)
        dw_tab = load_words(dict_pool.tile([P, G], I32, name="dw_tab", align_bytes=64, offset=0), d_words)
        ci_t = load_list("ci_t", ci)
        ds_tab = dict_pool.tile([P, G], U8, name="ds_tab", align_bytes=64, offset=4 * G)
        load_scales(ds_tab, d_scales, nc.vector.memset)
        n1_t = load_list("n1_t", n1)
        w_raw = keep.tile([P, 2, PACK, N], F32, name="w_raw")
        load_weight(w_raw[:, 0], w1)
        n2_t = load_list("n2_t", n2)
        load_weight(w_raw[:, 1], w2)
        n3_t = load_list("n3_t", n3)
        n4_t = load_list("n4_t", n4)
        n5_t = load_list("n5_t", n5)
        sl_t = load_by_slot("sl_t", sl)
        th_t = load_by_slot("th_t", th)
        gn_t = load_by_slot("gn_t", gn)

        warm = keep.tile([P, 2], F32, name="warm")
        nc.vector.memset(warm[:, 0:1], 0.0)
        nc.scalar.activation(warm[:, 1:2], warm[:, 0:1], ACT.Sigmoid)

        neg_sl = keep.tile([P, PACK], F32, name="neg_sl")
        bias = keep.tile([P, PACK], F32, name="bias")
        nc.scalar.activation(neg_sl[:], sl_t[:], ACT.Copy, scale=-1.0)
        for t in range(PACK):
            nc.scalar.activation(bias[:, t : t + 1], th_t[:, t : t + 1], ACT.Copy, scale=neg_sl[:, t : t + 1])

        def mx_tiles(name, width):
            words = keep.tile([P, width], U32, name=name + "_w", align_bytes=64)
            scales = keep.tile([P, width], U8, name=name + "_s", align_bytes=64)
            return words, scales

        def pick_words(dst, tab, lst):
            nc.vector.tensor_copy(dst, tab[:].bitcast(U32).indirect(lst[:]))

        def pick_scales(dst, tab, lst):
            nc.vector.tensor_copy(dst, tab[:].indirect(lst[:]))

        def dealt(tile):
            return tile[:].rearrange("q (t p) -> q p t", t=PACK)

        xq_w, xq_s = mx_tiles("xq", S)
        dq_w, dq_s = mx_tiles("dq", H)
        x2_s = keep.tile([P, S], U8, name="x2_s", align_bytes=64)
        pick_scales(xq_s[:], xs_tab, offs_t)
        pick_words(xq_w[:], xw_tab, offs_t)
        pick_scales(x2_s[:], xs_tab, two_t)
        pick_words(dealt(dq_w), dw_tab, ci_t)
        pick_scales(dealt(dq_s), ds_tab, ci_t)

        s_ps = [psum.tile([P, S], F32, name="s_ps%d" % t) for t in range(PACK)]
        for t in range(PACK):
            cols = slice(t * P, (t + 1) * P)
            nc.tensor.matmul_mx(
                s_ps[t][:], dq_w[:, cols].bitcast(FP8X4), dq_s[:, cols], xq_w[:].bitcast(FP8X4), xq_s[:],
                start=True, stop=True,
            )

        x2_w = dict_pool.tile([P, S], U32, name="x2_w", align_bytes=64, offset=4 * G - ROW_BYTES // 2)
        pick_words(x2_w[:], xw_tab, two_t)

        def quantize(name, woven, width):
            words, scales = mx_tiles(name, width)
            nc.vector.quantize_mx(words[:].bitcast(FP8X4), scales[:], woven)
            return words, scales

        def on_scalar(dst, src):
            nc.scalar.activation(dst, src, ACT.Copy)

        on_vector = nc.vector.tensor_copy

        def score_tile(name, shape, dtype, place):
            return score_pool.tile(shape, dtype, name=name, align_bytes=64, offset=place * ROW_BYTES)

        s_sb = [score_tile("s_sb%d" % t, [P, S], F32, t) for t in range(PACK)]
        gs_sb = [keep.tile([P, S], F32, name="gs_sb%d" % t) for t in range(PACK)]
        sg = [[keep.tile([P, HALF], F32, name="sg%d_%d" % (c, t)) for t in range(PACK)] for c in range(2)]
        z32 = [keep.tile([P, PACK, HALF], F32, name="z32_%d" % c) for c in range(2)]

        def gate(c, t):
            nc.scalar.activation(
                sg[c][t][:], s_sb[t][:].indirect(half_of(n1_t, c)), ACT.Sigmoid,
                bias=bias[:, t : t + 1], scale=sl_t[:, t : t + 1],
            )

        def gated_score(c, t):
            nc.vector.tensor_tensor(z32[c][:, t, :], gs_sb[t][:].indirect(half_of(n2_t, c)), sg[c][t][:], ALU.mult)

        def round_z(c, z16):
            on_vector(
                z16[:].rearrange("p (g i) t -> p g t i", i=LINE), z32[c][:].rearrange("p t (g i) -> p g t i", i=LINE)
            )

        w16_place = [PACK + m if m < W1_TILES_ON_VECTOR else m for m in range(ROW_TILES)]
        w16 = [score_tile("w16_%d" % m, [P, 2, P, PACK], BF16, w16_place[m]) for m in range(ROW_TILES)]
        h_ps = [psum.tile([P, S], F32, name="h_ps%d" % m) for m in range(ROW_TILES)]
        wq = []

        def round_weights(m, which, copy):
            copy(
                w16[m][:, which].rearrange("p w (g i) t -> p w g t i", i=LINE),
                w_raw[:, which, :, m * P : (m + 1) * P].rearrange("p w t (g i) -> p w g t i", i=LINE),
            )

        only_w1, only_w2, both = slice(0, 1), slice(1, 2), slice(0, 2)
        for m in range(W1_TILES_ON_VECTOR):
            round_weights(m, only_w1, on_vector)

        for t in range(PACK):
            nc.scalar.activation(s_sb[t][:], s_ps[t][:], ACT.Copy, scale=0.0625)
            gate(0, t)
            nc.vector.tensor_scalar(gs_sb[t][:], s_sb[t][:], gn_t[:, t : t + 1], None, ALU.mult)
            gated_score(0, t)

        z16_lo = keep.tile([P, HALF, PACK], BF16, name="z16_lo", align_bytes=64)
        round_z(0, z16_lo)
        gate(1, 0)
        gated_score(1, 0)
        zq = [quantize("zq0", z16_lo[:].rearrange("p j t -> p (j t)"), HALF)]
        for t in range(1, PACK):
            gate(1, t)
            gated_score(1, t)

        def w1_pass(m, c):
            words, scales = wq[m]
            nc.tensor.matmul_mx(
                h_ps[m][:, c * HALF : (c + 1) * HALF], words[:, :P].bitcast(FP8X4), scales[:, :P],
                zq[c][0][:].bitcast(FP8X4), zq[c][1][:], start=False, stop=(c == 1),
            )

        def open_group(m):
            wq.append(quantize("wq%d" % m, w16[m][:].rearrange("p w c t -> p (w c t)"), 2 * P))
            words, scales = wq[m]
            nc.tensor.matmul_mx(
                h_ps[m][:], words[:, P:].bitcast(FP8X4), scales[:, P:], x2_w[:].bitcast(FP8X4), x2_s[:],
                start=True, stop=False,
            )
            w1_pass(m, 0)

        for m in range(ROW_TILES):
            round_weights(m, only_w2 if m < W1_TILES_ON_VECTOR else both, nc.scalar.copy)
        open_group(0)
        z16_hi = score_tile("z16_hi", [P, HALF, PACK], BF16, w16_place[0])
        round_z(1, z16_hi)
        zq.append(quantize("zq1", z16_hi[:].rearrange("p j t -> p (j t)"), HALF))
        w1_pass(0, 1)
        last = ROW_TILES - 1
        for m in range(1, last):
            open_group(m)
            w1_pass(m, 1)

        early, late = range(2), range(2, ROW_TILES)
        ds = [keep.tile([P, S], F32, name="ds%d" % m) for m in early]
        ds = ds + [pair_pool.tile([P, S], F32, name="ds%d" % m, offset=(m - 2) * ROW_BYTES) for m in late]
        res = [keep.tile([P, S], F32, name="res%d" % m) for m in range(ROW_TILES)]
        pa = [pair_pool.tile([P, W], F32, name="pa%d" % m, offset=m * ROW_BYTES) for m in early]
        pb = [pair_pool.tile([P, W], F32, name="pb%d" % m, offset=2 * ROW_BYTES) for m in early]
        pa = pa + [keep.tile([P, W], F32, name="pa%d" % m) for m in late]
        pb = pb + [keep.tile([P, W], F32, name="pb%d" % m) for m in late]
        ra = [keep.tile([P, W], F32, name="ra%d" % m) for m in range(ROW_TILES)]
        neg_ds = [keep.tile([P, S], F32, name="neg_ds%d" % m) for m in range(last)]
        ds_n5 = keep.tile([P, S], F32, name="ds_n5")
        halves = [slice(c * HALF, (c + 1) * HALF) for c in range(2)]

        def put_back(m):
            on_scalar(ds[m][:].indirect(n3_t[:]), ra[m][:])

        def store(m, cols):
            nc.sync.dma_start(out[m * P : (m + 1) * P, cols], res[m][:, cols])

        on_vector(ds[0][:], h_ps[0][:])
        open_group(last)
        w1_pass(last, 1)
        for m in range(ROW_TILES):
            on_scalar(pa[m][:], ds[m][:].indirect(n3_t[:]))
            if m > 0:
                put_back(m - 1)
            if m < last:
                copy = nc.scalar.copy if m == 0 else on_vector
                copy(ds[m + 1][:], h_ps[m + 1][:])
            on_vector(pb[m][:], ds[m][:].indirect(n4_t[:]))
            nc.vector.tensor_tensor(ra[m][:], pa[m][:], pb[m][:], ALU.max)
        put_back(last)

        for m in range(last):
            nc.vector.tensor_scalar(neg_ds[m][:], ds[m][:], -1.0, None, ALU.mult)
            for c in range(2):
                nc.vector.tensor_tensor(
                    res[m][:, halves[c]], neg_ds[m][:].indirect(half_of(n5_t, c)), ds[m][:, halves[c]], ALU.add
                )
            store(m, slice(0, S))
        for c in range(2):
            on_scalar(ds_n5[:, halves[c]], ds[last][:].indirect(half_of(n5_t, c)))
            nc.vector.tensor_tensor(res[last][:, halves[c]], ds[last][:, halves[c]], ds_n5[:, halves[c]], ALU.subtract)
            store(last, halves[c])
